import numpy as np
import ml_dtypes


def mxq(x, axis, fmt="e4m3"):
    dtype, down = {"e4m3": (ml_dtypes.float8_e4m3fn, 7), "e5m2": (ml_dtypes.float8_e5m2, 14)}[fmt]
    v = np.moveaxis(np.asarray(x, np.float32).astype(ml_dtypes.bfloat16).astype(np.float64), axis, -1)
    blocks = v.reshape(v.shape[:-1] + (-1, 32))
    amax = np.abs(blocks).max(-1, keepdims=True)
    byte = np.maximum(np.where(amax > 0, np.frexp(amax)[1] - 1 + 127, 0) - down, 1)
    scale = np.exp2(byte - 127.0)
    codes = (blocks / scale).astype(np.float32).astype(dtype).astype(np.float64)
    return np.moveaxis((codes * scale).reshape(v.shape), -1, axis)


WIDE = False


def mx_kscale(k):
    if not WIDE:
        return np.ones(k)
    levels = np.array([10, -10, 5, -5, 0])
    if k % 512:
        return np.exp2(np.random.permutation(np.resize(levels, k // 32))).repeat(32)
    a = np.empty((k // 512, 16))
    for p in range(k // 512):
        a[p, :8] = np.random.permutation(np.resize(levels, 8))
        for g in range(8):
            far = levels[np.abs(levels - a[p, g]) >= 10]
            a[p, g + 8] = far[np.random.randint(len(far))]
    return np.exp2(a.ravel()).repeat(32)


def f64(x):
    return np.asarray(x).astype(np.float64)


def striped(idx):
    return np.tile(idx.reshape(-1, 16).T, (8, 1)).astype(np.uint16)


def unstriped(offs):
    return offs[:16].T.reshape(-1).astype(np.int64)


def striped8(idx):
    return np.concatenate([x.reshape(-1, 16).T for x in idx]).astype(np.uint16)


def runs(offs, k):
    lists = np.stack([offs[16 * r : 16 * r + 16].T.reshape(-1) for r in range(8)]).astype(np.int64)
    return lists[np.arange(k) % 512 // 64]


def pack_weight(w):
    k, n = w.shape
    w = f64(np.asarray(w, np.float32).astype(ml_dtypes.bfloat16)).reshape(k // 32, 32, n)
    amax = np.abs(w).max(1)
    byte = np.clip(np.where(amax > 0, np.frexp(amax)[1] - 1 + 127 - 7, 1), 1, 254)
    scaled = (w * np.exp2(127.0 - byte)[:, None, :]).reshape(k, n).astype(np.float32)
    words = np.ascontiguousarray(scaled.reshape(k // 512, 128, 4, n).transpose(0, 1, 3, 2)).astype(ml_dtypes.float8_e4m3fn).view(np.uint8)
    return words, np.ascontiguousarray(byte.astype(np.uint8).reshape(k // 512, 16, n))


def unpack_weight(words, scales):
    g, p, n, _ = words.shape
    vals = np.ascontiguousarray(words).view(ml_dtypes.float8_e4m3fn).astype(np.float64) * np.repeat(np.exp2(scales.astype(np.float64) - 127.0), 8, axis=1)[..., None]
    return vals.transpose(0, 1, 3, 2).reshape(g * 512, n)

def planes(y):
    n, m = y.shape
    v = y.astype(np.float32).astype(ml_dtypes.bfloat16).astype(np.float64).reshape(n // 32, 32, m)
    top = np.abs(v).max(1)
    byte = np.clip(np.where(top > 0, np.frexp(top)[1] - 1 + 127 - 7, 1), 1, 254)
    codes = (v * np.exp2(127.0 - byte)[:, None, :]).reshape(n, m).astype(np.float32).astype(ml_dtypes.float8_e4m3fn).view(np.uint8)
    words = codes.reshape(n // 512, 128, 4, m).transpose(0, 1, 3, 2)
    return np.ascontiguousarray(words), np.ascontiguousarray(byte.astype(np.uint8).reshape(n // 512, 16, m))


K, T, S, G, H, U = 512, 1024, 256, 2048, 512, 1024


def setup_inputs():
    n = np.random.standard_normal
    s = mx_kscale(K)[:, None]
    packed_xT = pack_weight(n((K, T)) * s)
    packed_dT = pack_weight(n((K, G)) / s)
    return {
        "x_words": packed_xT[0],
        "x_scales": packed_xT[1],
        "d_words": packed_dT[0],
        "d_scales": packed_dT[1],
        "gs": (np.random.uniform(0.5, 1.5, (K, 1)) * s).astype(np.float32),
        "offs": striped8(np.random.randint(0, T, (8, S))),
        "k1": striped8(np.random.randint(0, G, (8, H))),
        "hz": striped8(np.random.randint(0, T, (8, S))),
        "k2": striped8(np.random.randint(0, G, (8, H))),
        "n1": striped(np.random.permutation(S)),
        "n2": striped(np.random.permutation(S)),
        "n3": striped(np.random.permutation(S)),
        "k3": striped8(np.random.randint(0, G, (8, H))),
        "n4": striped(np.random.permutation(U)[:S]),
        "n5": striped(np.random.permutation(S)),
    }


def reference(x_words, x_scales, d_words, d_scales, gs, offs, k1, hz, k2, n1, n2, n3, k3, n4, n5):
    d_k3 = unpack_weight(d_words, d_scales)[np.arange(K)[:, None], runs(k3, K)]
    d_k1 = unpack_weight(d_words, d_scales)[np.arange(K)[:, None], runs(k1, K)]
    xq = unpack_weight(x_words, x_scales)[np.arange(K)[:, None], runs(offs, K)]
    d_k2 = unpack_weight(d_words, d_scales)[np.arange(K)[:, None], runs(k2, K)]
    x_hz = unpack_weight(x_words, x_scales)[np.arange(K)[:, None], runs(hz, K)]
    h = 0.0625 * (d_k1.T @ xq + d_k2.T @ x_hz)
    ds = np.zeros((H, S))
    ds[:, unstriped(n1)] = h
    st = np.minimum(ds, h[:, unstriped(n2)])
    z = f64(gs) * (st - st[:, unstriped(n3)])
    h2 = 0.0625 * ((d_k3.T @ mxq(z, 0, "e4m3")))
    nw = np.maximum(h2, h2[:, unstriped(n5)])
    out = np.zeros((H, U))
    out[:, unstriped(n4)] = nw
    return (out,) + planes(out)

@@ -1,0 +1,226 @@
+from contextlib import ExitStack
+
+import concourse.mybir as mybir
+
+K, T, S, G, H, U = 512, 1024, 256, 2048, 512, 1024
+FLOPS = 3 * 2 * K * H * S
+
+F32 = mybir.dt.float32
+BF16 = mybir.dt.bfloat16
+I32 = mybir.dt.int32
+U32 = mybir.dt.uint32
+U16 = mybir.dt.uint16
+U8 = mybir.dt.uint8
+FP8X4 = mybir.dt.float8_e4m3fn_x4
+ALU = mybir.AluOpType
+COPY = mybir.ActivationFunctionType.Copy
+
+P = 128
+PACK = 4
+GATHER_W = S + 16
+SCATTER_W = 2 * S
+SIXTEENTH = 0.0625
+
+
+def tile_picked_mhhzqsndminpags_none_po_kernel(
+    tc, x_words, x_scales, d_words, d_scales, gs, offs, k1, hz, k2, n1, n2, n3, k3, n4, n5, out_0, out_1, out_2
+):
+    nc = tc.nc
+    with ExitStack() as ctx:
+        sb = ctx.enter_context(tc.tile_pool(name="sb", bufs=1))
+        ps = ctx.enter_context(tc.psum_pool(name="ps", bufs=1))
+
+        def load_list(src, name):
+            lst = sb.tile(list(src.shape), U16, name=name)
+            nc.sync.dma_start(lst[:], src)
+            return lst
+
+        def load_words(src, width, name):
+            tab = sb.tile([P, width], I32, name=name, align_bytes=64)
+            nc.sync.dma_start(tab[:], src[0].rearrange("p c r -> p (c r)").bitcast(I32))
+            return tab
+
+        def load_scales(src, width, name):
+            tab = sb.tile([P, width], U8, name=name, align_bytes=64)
+            nc.vector.memset(tab[:].bitcast(I32), 0)
+            nc.scalar.dma_start(tab[0:P:8, :].bitcast(I32), src[0].bitcast(I32))
+            return tab
+
+        def zeroed_bytes(width, name):
+            tile = sb.tile([P, width], U8, name=name, align_bytes=64)
+            nc.gpsimd.memset(tile[:].bitcast(I32), 0)
+            return tile
+
+        def place_scale_rows(dst, src, queues):
+            for r in range(PACK):
+                queue = queues[r % len(queues)]
+                queue.dma_start(dst[r:P:32, :].bitcast(I32), src[8 * r : P : 32, :].bitcast(I32))
+
+        def deal(dst, src, line):
+            nc.vector.tensor_copy(
+                dst.rearrange("p (a t m i) -> p a m t i", t=PACK, m=P // line, i=line),
+                src.rearrange("p (a m i t) -> p a m t i", t=PACK, m=P // line, i=line),
+            )
+
+        d_scale_tab = load_scales(d_scales, G, "d_scale_tab")
+        x_scale_tab = load_scales(x_scales, T, "x_scale_tab")
+        k1_l = load_list(k1, "k1_l")
+        k2_l = load_list(k2, "k2_l")
+        offs_l = load_list(offs, "offs_l")
+        hz_l = load_list(hz, "hz_l")
+        d_tab = load_words(d_words, G, "d_tab")
+        x_tab = load_words(x_words, T, "x_tab")
+        gs_t = sb.tile([P, PACK], F32, name="gs_t")
+        nc.sync.dma_start(gs_t[:], gs.rearrange("(p t) o -> p (t o)", t=PACK))
+        n1_l = load_list(n1, "n1_l")
+        n2_l = load_list(n2, "n2_l")
+        n3_l = load_list(n3, "n3_l")
+        k3_l = load_list(k3, "k3_l")
+        n5_l = load_list(n5, "n5_l")
+        n4_l = load_list(n4, "n4_l")
+        gs16 = sb.tile([P, PACK], F32, name="gs16")
+        nc.scalar.activation(gs16[:], gs_t[:], COPY, scale=SIXTEENTH)
+
+        w12_sc = zeroed_bytes(2 * H, "w12_sc")
+        x_sc = zeroed_bytes(2 * S, "x_sc")
+        w3_sc = zeroed_bytes(H, "w3_sc")
+        page = []
+        for t in range(PACK):
+            tile = sb.tile([P, U], F32, name="page%d" % t)
+            nc.vector.memset(tile[:], 0.0)
+            page.append(tile)
+
+        b12 = sb.tile([P, 2 * H], U8, name="b12", align_bytes=64)
+        nc.vector.tensor_copy(b12[:, 0:H], d_scale_tab[:].indirect(k1_l[:]))
+        nc.vector.tensor_copy(b12[:, H : 2 * H], d_scale_tab[:].indirect(k2_l[:]))
+        bx = sb.tile([P, 2 * S], U8, name="bx", align_bytes=64)
+        nc.vector.tensor_copy(bx[:, 0:S], x_scale_tab[:].indirect(offs_l[:]))
+        b12_dealt = sb.tile([P, 2 * H], U8, name="b12_dealt", align_bytes=64)
+        deal(b12_dealt[:], b12[:], 16)
+        nc.vector.tensor_copy(bx[:, S : 2 * S], x_scale_tab[:].indirect(hz_l[:]))
+        place_scale_rows(w12_sc, b12_dealt, (nc.sync, nc.scalar))
+        place_scale_rows(x_sc, bx, (nc.sync, nc.scalar))
+
+        g12 = sb.tile([P, 2 * H], U32, name="g12", align_bytes=64)
+        nc.vector.tensor_copy(g12[:, 0:H], d_tab[:].bitcast(U32).indirect(k1_l[:]))
+        nc.vector.tensor_copy(g12[:, H : 2 * H], d_tab[:].bitcast(U32).indirect(k2_l[:]))
+        gx = sb.tile([P, 2 * S], U32, name="gx", tag="picked", align_bytes=64)
+        nc.vector.tensor_copy(gx[:, 0:S], x_tab[:].bitcast(U32).indirect(offs_l[:]))
+        w12 = sb.tile([P, 2 * H], U32, name="w12", align_bytes=64)
+        deal(w12[:], g12[:], 4)
+        nc.vector.tensor_copy(gx[:, S : 2 * S], x_tab[:].bitcast(U32).indirect(hz_l[:]))
+
+        acc = []
+        for t in range(PACK):
+            bank = ps.tile([P, S], F32, name="h_acc%d" % t)
+            for a in range(2):
+                cols = slice(a * H + t * P, a * H + (t + 1) * P)
+                toks = slice(a * S, (a + 1) * S)
+                nc.tensor.matmul_mx(
+                    out=bank[:],
+                    lhsT=w12[:, cols].bitcast(FP8X4),
+                    lhsT_scale=w12_sc[:, cols],
+                    rhs=gx[:, toks].bitcast(FP8X4),
+                    rhs_scale=x_sc[:, toks],
+                    start=(a == 0),
+                    stop=(a == 1),
+                )
+            acc.append(bank)
+        h = []
+        for t in range(PACK):
+            tile = sb.tile([P, GATHER_W], F32, name="h%d" % t)
+            nc.vector.tensor_copy(tile[:, 0:S], acc[t][:])
+            h.append(tile)
+
+        b3 = sb.tile([P, H], U8, name="b3", tag="x_sc", align_bytes=64)
+        g3 = sb.tile([P, H], U32, name="g3", tag="picked", align_bytes=64)
+        b3_dealt = sb.tile([P, H], U8, name="b3_dealt", align_bytes=64)
+        w3 = sb.tile([P, H], U32, name="w3", align_bytes=64)
+
+        z_in = sb.tile([P, S, PACK], BF16, name="z_in", align_bytes=64)
+        stw = {}
+
+        def first_step(t):
+            ds = sb.tile([P, SCATTER_W], F32, name="ds%d" % t)
+            nc.scalar.activation(ds[:].indirect(n1_l[:]), h[t][:, 0:S], COPY)
+            far = sb.tile([P, S], F32, name="h_n2_%d" % t)
+            nc.scalar.activation(far[:], h[t][:].indirect(n2_l[:]), COPY)
+            st = sb.tile([P, S], F32, name="st%d" % t)
+            nc.vector.tensor_tensor(st[:], ds[:, 0:S], far[:], ALU.min)
+            tile = sb.tile([P, GATHER_W], F32, name="stw%d" % t)
+            nc.vector.tensor_scalar(tile[:, 0:S], st[:], gs16[:, t : t + 1], None, ALU.mult)
+            stw[t] = tile
+
+        def second_step(t):
+            far = sb.tile([P, S], F32, name="st_n3_%d" % t)
+            nc.scalar.activation(far[:], stw[t][:].indirect(n3_l[:]), COPY)
+            nc.vector.tensor_tensor(z_in[:, :, t], stw[t][:, 0:S], far[:], ALU.subtract)
+
+        first_step(0)
+        for half in range(2):
+            cols = slice(half * S, (half + 1) * S)
+            nc.vector.tensor_copy(b3[:, cols], d_scale_tab[:].indirect(k3_l[:, 16 * half : 16 * (half + 1)]))
+        deal(b3_dealt[:], b3[:], 16)
+        place_scale_rows(w3_sc, b3_dealt, (nc.sync,))
+        first_step(1)
+        second_step(0)
+        for half in range(2):
+            cols = slice(half * S, (half + 1) * S)
+            nc.vector.tensor_copy(g3[:, cols], d_tab[:].bitcast(U32).indirect(k3_l[:, 16 * half : 16 * (half + 1)]))
+        deal(w3[:], g3[:], 4)
+        first_step(2)
+        second_step(1)
+        first_step(3)
+        second_step(2)
+        second_step(3)
+
+        z_words = sb.tile([P, S], U32, name="z_words", align_bytes=64)
+        z_sc = sb.tile([P, S], U8, name="z_sc", align_bytes=64)
+        nc.vector.quantize_mx(out=z_words[:].bitcast(FP8X4), scales=z_sc[:], in_=z_in[:].rearrange("p c t -> p (c t)"))
+
+        nw = []
+        for t in range(PACK):
+            bank = ps.tile([P, S], F32, name="h2_acc%d" % t)
+            cols = slice(t * P, (t + 1) * P)
+            nc.tensor.matmul_mx(
+                out=bank[:],
+                lhsT=w3[:, cols].bitcast(FP8X4),
+                lhsT_scale=w3_sc[:, cols],
+                rhs=z_words[:].bitcast(FP8X4),
+                rhs_scale=z_sc[:],
+                start=True,
+                stop=True,
+            )
+            h2 = sb.tile([P, GATHER_W], F32, name="h2_%d" % t)
+            nc.vector.tensor_scalar(h2[:, 0:S], bank[:], SIXTEENTH, None, ALU.mult)
+            far = sb.tile([P, S], F32, name="h2_n5_%d" % t)
+            nc.scalar.activation(far[:], h2[:].indirect(n5_l[:]), COPY)
+            tile = sb.tile([P, S], F32, name="nw%d" % t)
+            nc.vector.tensor_tensor(tile[:], h2[:, 0:S], far[:], ALU.max)
+            nw.append(tile)
+
+        y_in = sb.tile([P, U, PACK], BF16, name="y_in", align_bytes=64)
+        y_words = sb.tile([P, U], I32, name="y_words", align_bytes=64)
+        y_sc = sb.tile([P, U], U8, name="y_sc", align_bytes=64)
+        out_rows = out_0.rearrange("(p t) c -> p t c", t=PACK)
+        out_words = out_1[0].rearrange("p c r -> p (c r)").bitcast(I32)
+        for t in range(PACK):
+            nc.scalar.activation(page[t][:].indirect(n4_l[:]), nw[t][:], COPY)
+            nc.sync.dma_start(out_rows[:, t, :], page[t][:])
+            if t < PACK - 1:
+                nc.vector.tensor_copy(y_in[:, :, t], page[t][:])
+        half_w = U // 2
+        for half in range(2):
+            cols = slice(half * half_w, (half + 1) * half_w)
+            nc.vector.tensor_copy(y_in[:, cols, PACK - 1], page[PACK - 1][:, cols])
+        for half in range(2):
+            cols = slice(half * half_w, (half + 1) * half_w)
+            nc.vector.quantize_mx(
+                out=y_words[:, cols].bitcast(FP8X4),
+                scales=y_sc[:, cols],
+                in_=y_in[:, cols, :].rearrange("p c t -> p (c t)"),
+            )
+            nc.sync.dma_start(out_words[:, cols], y_words[:, cols])
+        for q in range(4):
+            queue = nc.scalar if q % 2 == 0 else nc.sync
+            queue.dma_start(out_2[0][4 * q : 4 * q + 4, :].bitcast(I32), y_sc[32 * q : 32 * q + 4, :].bitcast(I32))

@@ -16,7 +16,9 @@ ALU = mybir.AluOpType
 COPY = mybir.ActivationFunctionType.Copy
 
 P = 128
+HALF_P = P // 2
 PACK = 4
+LINE = 16
 GATHER_W = S + 16
 SCATTER_W = 2 * S
 SIXTEENTH = 0.0625
@@ -42,179 +44,258 @@ def tile_picked_mhhzqsndminpags_none_po_kernel(
 
         def load_scales(src, width, name):
             tab = sb.tile([P, width], U8, name=name, align_bytes=64)
-            nc.vector.memset(tab[:].bitcast(I32), 0)
-            nc.scalar.dma_start(tab[0:P:8, :].bitcast(I32), src[0].bitcast(I32))
+            rows = src[0].bitcast(I32).unsqueeze(1).broadcast_to([16, 8, width // 4])
+            nc.scalar.dma_start(tab[:].bitcast(I32), rows)
             return tab
 
-        def zeroed_bytes(width, name):
-            tile = sb.tile([P, width], U8, name=name, align_bytes=64)
+        def zeroed_bytes(width, name, tag):
+            tile = sb.tile([P, width], U8, name=name, tag=tag, align_bytes=64)
             nc.gpsimd.memset(tile[:].bitcast(I32), 0)
             return tile
 
         def place_scale_rows(dst, src, queues):
             for r in range(PACK):
-                queue = queues[r % len(queues)]
-                queue.dma_start(dst[r:P:32, :].bitcast(I32), src[8 * r : P : 32, :].bitcast(I32))
+                queues[r % len(queues)].dma_start(dst[r:P:32, :].bitcast(I32), src[8 * r : P : 32, :].bitcast(I32))
 
-        def deal(dst, src, line):
+        def pick(dst, table, lst, first, count):
+            nc.vector.tensor_copy(dst, table.indirect(lst[:, first // 16 : (first + count) // 16]))
+
+        def deal(dst, src, run):
             nc.vector.tensor_copy(
-                dst.rearrange("p (a t m i) -> p a m t i", t=PACK, m=P // line, i=line),
-                src.rearrange("p (a m i t) -> p a m t i", t=PACK, m=P // line, i=line),
+                dst.rearrange("p a t (m i) -> p a m t i", i=run), src.rearrange("p a (m i) t -> p a m t i", i=run)
             )
 
-        d_scale_tab = load_scales(d_scales, G, "d_scale_tab")
         x_scale_tab = load_scales(x_scales, T, "x_scale_tab")
-        k1_l = load_list(k1, "k1_l")
-        k2_l = load_list(k2, "k2_l")
+        d_scale_tab = load_scales(d_scales, G, "d_scale_tab")
         offs_l = load_list(offs, "offs_l")
         hz_l = load_list(hz, "hz_l")
-        d_tab = load_words(d_words, G, "d_tab")
-        x_tab = load_words(x_words, T, "x_tab")
+        k1_l = load_list(k1, "k1_l")
+        k2_l = load_list(k2, "k2_l")
         gs_t = sb.tile([P, PACK], F32, name="gs_t")
         nc.sync.dma_start(gs_t[:], gs.rearrange("(p t) o -> p (t o)", t=PACK))
+        x_tab = load_words(x_words, T, "x_tab")
         n1_l = load_list(n1, "n1_l")
         n2_l = load_list(n2, "n2_l")
         n3_l = load_list(n3, "n3_l")
+        d_tab = load_words(d_words, G, "d_tab")
         k3_l = load_list(k3, "k3_l")
         n5_l = load_list(n5, "n5_l")
         n4_l = load_list(n4, "n4_l")
         gs16 = sb.tile([P, PACK], F32, name="gs16")
         nc.scalar.activation(gs16[:], gs_t[:], COPY, scale=SIXTEENTH)
+        minus_gs16 = sb.tile([P, PACK], F32, name="minus_gs16")
+        nc.scalar.activation(minus_gs16[:], gs_t[:], COPY, scale=-SIXTEENTH)
+        d_codes = d_tab[:].bitcast(U32)
+        x_codes = x_tab[:].bitcast(U32)
 
-        w12_sc = zeroed_bytes(2 * H, "w12_sc")
-        x_sc = zeroed_bytes(2 * S, "x_sc")
-        w3_sc = zeroed_bytes(H, "w3_sc")
+        h_sc = zeroed_bytes(2 * H + 2 * S, "h_sc", "h_sc")
+        w3_sc = zeroed_bytes(H, "w3_sc", "w3_sc")
         page = []
         for t in range(PACK):
             tile = sb.tile([P, U], F32, name="page%d" % t)
-            nc.vector.memset(tile[:], 0.0)
+            (nc.vector if t in (2, 0) else nc.gpsimd).memset(tile[:], 0.0)
             page.append(tile)
 
-        b12 = sb.tile([P, 2 * H], U8, name="b12", align_bytes=64)
-        nc.vector.tensor_copy(b12[:, 0:H], d_scale_tab[:].indirect(k1_l[:]))
-        nc.vector.tensor_copy(b12[:, H : 2 * H], d_scale_tab[:].indirect(k2_l[:]))
+        def deal_pair(dst, picked, pair, run):
+            deal(dst, picked[:, :, :, 2 * pair : 2 * pair + 2], run)
+
         bx = sb.tile([P, 2 * S], U8, name="bx", align_bytes=64)
-        nc.vector.tensor_copy(bx[:, 0:S], x_scale_tab[:].indirect(offs_l[:]))
-        b12_dealt = sb.tile([P, 2 * H], U8, name="b12_dealt", align_bytes=64)
-        deal(b12_dealt[:], b12[:], 16)
-        nc.vector.tensor_copy(bx[:, S : 2 * S], x_scale_tab[:].indirect(hz_l[:]))
-        place_scale_rows(w12_sc, b12_dealt, (nc.sync, nc.scalar))
-        place_scale_rows(x_sc, bx, (nc.sync, nc.scalar))
+        pick(bx[:, 0:S], x_scale_tab[:], offs_l, 0, S)
+        pick(bx[:, S : 2 * S], x_scale_tab[:], hz_l, 0, S)
+        b12 = sb.tile([P, 2 * H], U8, name="b12", align_bytes=64)
+        pick(b12[:, 0:H], d_scale_tab[:], k1_l, 0, H)
+        pick(b12[:, H : 2 * H], d_scale_tab[:], k2_l, 0, H)
+        h_b = sb.tile([P, 2 * H + 2 * S], U8, name="h_b", align_bytes=64)
+        nc.vector.tensor_copy(h_b[:, 2 * H :].bitcast(I32), bx[:].bitcast(I32))
+        deal_pair(
+            h_b[:, 0:H].rearrange("p (a t m) -> p a t m", a=4, t=2),
+            b12[:].rearrange("p (a m t) -> p a m t", a=4, t=PACK),
+            0,
+            LINE,
+        )
+        deal_pair(
+            h_b[:, H : 2 * H].rearrange("p (a t m) -> p a t m", a=2, t=2),
+            b12[:].rearrange("p (a m t) -> p a m t", a=2, t=PACK),
+            1,
+            LINE,
+        )
+        place_scale_rows(h_sc, h_b, (nc.sync, nc.scalar))
 
-        g12 = sb.tile([P, 2 * H], U32, name="g12", align_bytes=64)
-        nc.vector.tensor_copy(g12[:, 0:H], d_tab[:].bitcast(U32).indirect(k1_l[:]))
-        nc.vector.tensor_copy(g12[:, H : 2 * H], d_tab[:].bitcast(U32).indirect(k2_l[:]))
-        gx = sb.tile([P, 2 * S], U32, name="gx", tag="picked", align_bytes=64)
-        nc.vector.tensor_copy(gx[:, 0:S], x_tab[:].bitcast(U32).indirect(offs_l[:]))
-        w12 = sb.tile([P, 2 * H], U32, name="w12", align_bytes=64)
-        deal(w12[:], g12[:], 4)
-        nc.vector.tensor_copy(gx[:, S : 2 * S], x_tab[:].bitcast(U32).indirect(hz_l[:]))
+        gx = sb.tile([P, 2 * S], U32, name="gx", align_bytes=64)
+        pick(gx[:, 0:S], x_codes, offs_l, 0, S)
+        pick(gx[:, S : 2 * S], x_codes, hz_l, 0, S)
+        h_w = sb.tile([P, 2 * H], U32, name="h_w", align_bytes=64)
+        folded = h_w[:, 0:H].rearrange("p (a h t m) -> p a h t m", a=2, h=2, t=2)
+        plain = h_w[:, H : 2 * H].rearrange("p (a t h m) -> p a t h m", a=2, t=2, h=2)
 
-        acc = []
-        for t in range(PACK):
+        def pick_half(half):
+            tile = sb.tile([P, 2, HALF_P, PACK], U32, name="half_w", align_bytes=64)
+            flat = tile[:].rearrange("p a m t -> p (a m t)")
+            pick(flat[:, 0:S], d_codes, k1_l, half * S, S)
+            pick(flat[:, S : 2 * S], d_codes, k2_l, half * S, S)
+            deal_pair(folded[:, :, half, :, :], tile[:], 0, LINE // 4)
+            deal_pair(plain[:, :, :, half, :], tile[:], 1, LINE // 4)
+
+        def product(t):
             bank = ps.tile([P, S], F32, name="h_acc%d" % t)
             for a in range(2):
-                cols = slice(a * H + t * P, a * H + (t + 1) * P)
-                toks = slice(a * S, (a + 1) * S)
+                first = (t // 2) * H + (2 * a + t % 2) * P
                 nc.tensor.matmul_mx(
                     out=bank[:],
-                    lhsT=w12[:, cols].bitcast(FP8X4),
-                    lhsT_scale=w12_sc[:, cols],
-                    rhs=gx[:, toks].bitcast(FP8X4),
-                    rhs_scale=x_sc[:, toks],
+                    lhsT=h_w[:, first : first + P].bitcast(FP8X4),
+                    lhsT_scale=h_sc[:, first : first + P],
+                    rhs=gx[:, a * S : (a + 1) * S].bitcast(FP8X4),
+                    rhs_scale=h_sc[:, 2 * H + a * S : 2 * H + (a + 1) * S],
                     start=(a == 0),
                     stop=(a == 1),
                 )
-            acc.append(bank)
-        h = []
-        for t in range(PACK):
-            tile = sb.tile([P, GATHER_W], F32, name="h%d" % t)
-            nc.vector.tensor_copy(tile[:, 0:S], acc[t][:])
-            h.append(tile)
+            return bank
 
-        b3 = sb.tile([P, H], U8, name="b3", tag="x_sc", align_bytes=64)
-        g3 = sb.tile([P, H], U32, name="g3", tag="picked", align_bytes=64)
-        b3_dealt = sb.tile([P, H], U8, name="b3_dealt", align_bytes=64)
-        w3 = sb.tile([P, H], U32, name="w3", align_bytes=64)
+        h = [sb.tile([P, GATHER_W], F32, name="h%d" % t, align_bytes=64) for t in range(PACK)]
+        pick_half(0)
+        nc.scalar.copy(h[0][:, 0:S], product(0)[:])
+        pick_half(1)
+        for t in range(1, PACK):
+            nc.vector.tensor_copy(h[t][:, 0:S], product(t)[:])
+
+        ds, near, st = {}, {}, {}
+
+        def send_n1(t, tag):
+            ds[t] = sb.tile([P, SCATTER_W], F32, name="ds%d" % t, tag=tag, align_bytes=64)
+            nc.scalar.activation(ds[t][:].indirect(n1_l[:]), h[t][:, 0:S], COPY)
+
+        def fetch_n2(t, tag):
+            near[t] = sb.tile([P, S], F32, name="h_n2_%d" % t, tag=tag, align_bytes=64)
+            nc.scalar.activation(near[t][:], h[t][:].indirect(n2_l[:]), COPY)
+
+        def smaller(t, tag):
+            st[t] = sb.tile([P, GATHER_W], F32, name="st%d" % t, tag=tag, align_bytes=64)
+            nc.vector.tensor_tensor(st[t][:, 0:S], ds[t][:, 0:S], near[t][:], ALU.min)
+
+        def fetch_n3(t, first, count):
+            far = sb.tile([P, count], F32, name="st_n3_%d_%d" % (t, first), align_bytes=64)
+            nc.scalar.activation(far[:], st[t][:].indirect(n3_l[:, first // 16 : (first + count) // 16]), COPY)
+            return far
 
         z_in = sb.tile([P, S, PACK], BF16, name="z_in", align_bytes=64)
-        stw = {}
+        unfolded = sb.tile([P, 2, S], F32, name="unfolded", align_bytes=64)
 
-        def first_step(t):
-            ds = sb.tile([P, SCATTER_W], F32, name="ds%d" % t)
-            nc.scalar.activation(ds[:].indirect(n1_l[:]), h[t][:, 0:S], COPY)
-            far = sb.tile([P, S], F32, name="h_n2_%d" % t)
-            nc.scalar.activation(far[:], h[t][:].indirect(n2_l[:]), COPY)
-            st = sb.tile([P, S], F32, name="st%d" % t)
-            nc.vector.tensor_tensor(st[:], ds[:, 0:S], far[:], ALU.min)
-            tile = sb.tile([P, GATHER_W], F32, name="stw%d" % t)
-            nc.vector.tensor_scalar(tile[:, 0:S], st[:], gs16[:, t : t + 1], None, ALU.mult)
-            stw[t] = tile
+        def unfold(half):
+            diff = sb.tile([P, S], F32, name="diff%d" % half)
+            nc.vector.tensor_tensor(diff[:], st[half][:, 0:S], fetch_n3(half, 0, S)[:], ALU.subtract)
+            for t in range(2):
+                nc.sync.dma_start(
+                    unfolded[half * HALF_P : (half + 1) * HALF_P, t, :], diff[t * HALF_P : (t + 1) * HALF_P, :]
+                )
 
-        def second_step(t):
-            far = sb.tile([P, S], F32, name="st_n3_%d" % t)
-            nc.scalar.activation(far[:], stw[t][:].indirect(n3_l[:]), COPY)
-            nc.vector.tensor_tensor(z_in[:, :, t], stw[t][:, 0:S], far[:], ALU.subtract)
+        for t in range(2):
+            send_n1(t, "ds%d" % t)
+            fetch_n2(t, "near%d" % t)
+            smaller(t, "st%d" % t)
+        unfold(0)
+        unfold(1)
+        fetch_n2(2, "near2")
 
-        first_step(0)
+        b3 = sb.tile([P, 1, P, PACK], U8, name="b3", tag="ds0", align_bytes=64)
+        b3_flat = b3[:].rearrange("p a m t -> p (a m t)")
         for half in range(2):
-            cols = slice(half * S, (half + 1) * S)
-            nc.vector.tensor_copy(b3[:, cols], d_scale_tab[:].indirect(k3_l[:, 16 * half : 16 * (half + 1)]))
-        deal(b3_dealt[:], b3[:], 16)
+            pick(b3_flat[:, half * S : (half + 1) * S], d_scale_tab[:], k3_l, half * S, S)
+        b3_dealt = sb.tile([P, H], U8, name="b3_dealt", align_bytes=64)
+        deal(b3_dealt[:].rearrange("p (a t m) -> p a t m", a=1, t=PACK), b3[:], LINE)
         place_scale_rows(w3_sc, b3_dealt, (nc.sync,))
-        first_step(1)
-        second_step(0)
+
+        g3 = sb.tile([P, 1, P, PACK], U32, name="g3", tag="near1", align_bytes=64)
+        g3_flat = g3[:].rearrange("p a m t -> p (a m t)")
         for half in range(2):
-            cols = slice(half * S, (half + 1) * S)
-            nc.vector.tensor_copy(g3[:, cols], d_tab[:].bitcast(U32).indirect(k3_l[:, 16 * half : 16 * (half + 1)]))
-        deal(w3[:], g3[:], 4)
-        first_step(2)
-        second_step(1)
-        first_step(3)
-        second_step(2)
-        second_step(3)
+            pick(g3_flat[:, half * S : (half + 1) * S], d_codes, k3_l, half * S, S)
+        w3 = sb.tile([P, H], U32, name="w3", align_bytes=64)
+        deal(w3[:].rearrange("p (a t m) -> p a t m", a=1, t=PACK), g3[:], LINE // 4)
 
         z_words = sb.tile([P, S], U32, name="z_words", align_bytes=64)
         z_sc = sb.tile([P, S], U8, name="z_sc", align_bytes=64)
-        nc.vector.quantize_mx(out=z_words[:].bitcast(FP8X4), scales=z_sc[:], in_=z_in[:].rearrange("p c t -> p (c t)"))
+        order = (2, 0, 1, 3)
+        banks = {t: ps.tile([P, S], F32, name="h2_acc%d" % t) for t in order}
+        weighted = {}
 
-        nw = []
-        for t in range(PACK):
-            bank = ps.tile([P, S], F32, name="h2_acc%d" % t)
-            cols = slice(t * P, (t + 1) * P)
-            nc.tensor.matmul_mx(
-                out=bank[:],
-                lhsT=w3[:, cols].bitcast(FP8X4),
-                lhsT_scale=w3_sc[:, cols],
-                rhs=z_words[:].bitcast(FP8X4),
-                rhs_scale=z_sc[:],
-                start=True,
-                stop=True,
+        def weigh(t):
+            weighted[t] = sb.tile([P, S], F32, name="weighted%d" % t)
+            nc.vector.tensor_scalar(weighted[t][:], st[t][:, 0:S], gs16[:, t : t + 1], None, ALU.mult)
+
+        def finish_z(t, half):
+            toks = slice(half * P, (half + 1) * P)
+            nc.vector.scalar_tensor_tensor(
+                z_in[:, toks, t],
+                fetch_n3(t, half * P, P)[:],
+                minus_gs16[:, t : t + 1],
+                weighted[t][:, toks],
+                ALU.mult,
+                ALU.add,
             )
-            h2 = sb.tile([P, GATHER_W], F32, name="h2_%d" % t)
-            nc.vector.tensor_scalar(h2[:, 0:S], bank[:], SIXTEENTH, None, ALU.mult)
-            far = sb.tile([P, S], F32, name="h2_n5_%d" % t)
-            nc.scalar.activation(far[:], h2[:].indirect(n5_l[:]), COPY)
-            tile = sb.tile([P, S], F32, name="nw%d" % t)
-            nc.vector.tensor_tensor(tile[:], h2[:, 0:S], far[:], ALU.max)
-            nw.append(tile)
+
+        send_n1(2, "ds1")
+        smaller(2, "st2")
+        weigh(2)
+        fetch_n2(3, "h2")
+        finish_z(2, 0)
+        send_n1(3, "near2")
+        for t in range(2):
+            nc.vector.tensor_scalar(z_in[:, :, t], unfolded[:, t, :], gs16[:, t : t + 1], None, ALU.mult)
+        smaller(3, "unfolded")
+        weigh(3)
+        finish_z(2, 1)
+        finish_z(3, 0)
+        finish_z(3, 1)
+        for half in range(2):
+            toks = slice(half * P, (half + 1) * P)
+            nc.vector.quantize_mx(
+                out=z_words[:, toks].bitcast(FP8X4),
+                scales=z_sc[:, toks],
+                in_=z_in[:, toks, :].rearrange("p c t -> p (c t)"),
+            )
+        for t in order:
+            cols = slice(t * P, (t + 1) * P)
+            for half in range(2):
+                toks = slice(half * P, (half + 1) * P)
+                nc.tensor.matmul_mx(
+                    out=banks[t][:, toks],
+                    lhsT=w3[:, cols].bitcast(FP8X4),
+                    lhsT_scale=w3_sc[:, cols],
+                    rhs=z_words[:, toks].bitcast(FP8X4),
+                    rhs_scale=z_sc[:, toks],
+                    start=True,
+                    stop=True,
+                )
 
         y_in = sb.tile([P, U, PACK], BF16, name="y_in", align_bytes=64)
         y_words = sb.tile([P, U], I32, name="y_words", align_bytes=64)
         y_sc = sb.tile([P, U], U8, name="y_sc", align_bytes=64)
         out_rows = out_0.rearrange("(p t) c -> p t c", t=PACK)
         out_words = out_1[0].rearrange("p c r -> p (c r)").bitcast(I32)
-        for t in range(PACK):
+        nw = {}
+
+        def larger(t, tag):
+            h2 = sb.tile([P, GATHER_W], F32, name="h2_%d" % t)
+            nc.vector.tensor_scalar(h2[:, 0:S], banks[t][:], SIXTEENTH, None, ALU.mult)
+            far = sb.tile([P, S], F32, name="h2_n5_%d" % t, tag=tag)
+            nc.scalar.activation(far[:], h2[:].indirect(n5_l[:]), COPY)
+            nw[t] = sb.tile([P, S], F32, name="nw%d" % t)
+            nc.vector.tensor_tensor(nw[t][:], h2[:, 0:S], far[:], ALU.max)
+
+        larger(order[0], "far_a")
+        larger(order[1], "far_b")
+        for i, t in enumerate(order):
             nc.scalar.activation(page[t][:].indirect(n4_l[:]), nw[t][:], COPY)
             nc.sync.dma_start(out_rows[:, t, :], page[t][:])
-            if t < PACK - 1:
+            if t != order[-1]:
                 nc.vector.tensor_copy(y_in[:, :, t], page[t][:])
-        half_w = U // 2
-        for half in range(2):
-            cols = slice(half * half_w, (half + 1) * half_w)
-            nc.vector.tensor_copy(y_in[:, cols, PACK - 1], page[PACK - 1][:, cols])
-        for half in range(2):
-            cols = slice(half * half_w, (half + 1) * half_w)
+            if i + 2 < PACK:
+                larger(order[i + 2], "nw%d" % t)
+        last = order[-1]
+        pieces = (slice(0, U // 2), slice(U // 2, 3 * U // 4), slice(3 * U // 4, U))
+        nc.vector.tensor_copy(y_in[:, pieces[0], last], page[last][:, pieces[0]])
+        for cols in pieces[1:]:
+            nc.scalar.copy(y_in[:, cols, last], page[last][:, cols])
+        for cols in pieces:
             nc.vector.quantize_mx(
                 out=y_words[:, cols].bitcast(FP8X4),
                 scales=y_sc[:, cols],

@@ -50,7 +50,7 @@ def tile_picked_mhhzqsndminpags_none_po_kernel(
 
         def zeroed_bytes(width, name, tag):
             tile = sb.tile([P, width], U8, name=name, tag=tag, align_bytes=64)
-            nc.gpsimd.memset(tile[:].bitcast(I32), 0)
+            nc.vector.memset(tile[:].bitcast(I32), 0)
             return tile
 
         def place_scale_rows(dst, src, queues):
@@ -90,11 +90,14 @@ def tile_picked_mhhzqsndminpags_none_po_kernel(
 
         h_sc = zeroed_bytes(2 * H + 2 * S, "h_sc", "h_sc")
         w3_sc = zeroed_bytes(H, "w3_sc", "w3_sc")
-        page = []
-        for t in range(PACK):
-            tile = sb.tile([P, U], F32, name="page%d" % t)
-            (nc.vector if t in (2, 0) else nc.gpsimd).memset(tile[:], 0.0)
-            page.append(tile)
+        page = {}
+
+        def clear_page(t, tag):
+            page[t] = sb.tile([P, U], F32, name="page%d" % t, tag=tag, align_bytes=64)
+            nc.vector.memset(page[t][:], 0.0)
+
+        clear_page(2, "page2")
+        clear_page(0, "page0")
 
         def deal_pair(dst, picked, pair, run):
             deal(dst, picked[:, :, :, 2 * pair : 2 * pair + 2], run)
@@ -178,6 +181,7 @@ def tile_picked_mhhzqsndminpags_none_po_kernel(
             return far
 
         z_in = sb.tile([P, S, PACK], BF16, name="z_in", align_bytes=64)
+        z_planes = sb.tile([P, PACK, S], BF16, name="z_planes", align_bytes=64)
         unfolded = sb.tile([P, 2, S], F32, name="unfolded", align_bytes=64)
 
         def unfold(half):
@@ -194,7 +198,6 @@ def tile_picked_mhhzqsndminpags_none_po_kernel(
             smaller(t, "st%d" % t)
         unfold(0)
         unfold(1)
-        fetch_n2(2, "near2")
 
         b3 = sb.tile([P, 1, P, PACK], U8, name="b3", tag="ds0", align_bytes=64)
         b3_flat = b3[:].rearrange("p a m t -> p (a m t)")
@@ -217,15 +220,15 @@ def tile_picked_mhhzqsndminpags_none_po_kernel(
         banks = {t: ps.tile([P, S], F32, name="h2_acc%d" % t) for t in order}
         weighted = {}
 
-        def weigh(t):
-            weighted[t] = sb.tile([P, S], F32, name="weighted%d" % t)
+        def weigh(t, tag):
+            weighted[t] = sb.tile([P, S], F32, name="weighted%d" % t, tag=tag, align_bytes=64)
             nc.vector.tensor_scalar(weighted[t][:], st[t][:, 0:S], gs16[:, t : t + 1], None, ALU.mult)
 
-        def finish_z(t, half):
-            toks = slice(half * P, (half + 1) * P)
+        def finish_z(t, first, count):
+            toks = slice(first, first + count)
             nc.vector.scalar_tensor_tensor(
-                z_in[:, toks, t],
-                fetch_n3(t, half * P, P)[:],
+                z_planes[:, t, toks],
+                fetch_n3(t, first, count)[:],
                 minus_gs16[:, t : t + 1],
                 weighted[t][:, toks],
                 ALU.mult,
@@ -233,18 +236,25 @@ def tile_picked_mhhzqsndminpags_none_po_kernel(
             )
 
         send_n1(2, "ds1")
+        fetch_n2(2, "near2")
         smaller(2, "st2")
-        weigh(2)
-        fetch_n2(3, "h2")
-        finish_z(2, 0)
-        send_n1(3, "near2")
+        clear_page(1, "near2")
+        send_n1(3, "h2")
+        fetch_n2(3, "near3")
         for t in range(2):
-            nc.vector.tensor_scalar(z_in[:, :, t], unfolded[:, t, :], gs16[:, t : t + 1], None, ALU.mult)
+            nc.vector.tensor_scalar(z_planes[:, t, :], unfolded[:, t, :], gs16[:, t : t + 1], None, ALU.mult)
         smaller(3, "unfolded")
-        weigh(3)
-        finish_z(2, 1)
-        finish_z(3, 0)
-        finish_z(3, 1)
+        weigh(2, "near3")
+        weigh(3, "weighted3")
+        finish_z(2, 0, S)
+        finish_z(3, 0, P)
+        finish_z(3, P, P)
+        for half in range(2):
+            toks = slice(half * P, (half + 1) * P)
+            nc.vector.tensor_copy(
+                z_in[:, toks, :].rearrange("p (c i) t -> p c t i", i=4),
+                z_planes[:, :, toks].rearrange("p t (c i) -> p c t i", i=4),
+            )
         for half in range(2):
             toks = slice(half * P, (half + 1) * P)
             nc.vector.quantize_mx(
@@ -276,13 +286,14 @@ def tile_picked_mhhzqsndminpags_none_po_kernel(
         def larger(t, tag):
             h2 = sb.tile([P, GATHER_W], F32, name="h2_%d" % t)
             nc.vector.tensor_scalar(h2[:, 0:S], banks[t][:], SIXTEENTH, None, ALU.mult)
-            far = sb.tile([P, S], F32, name="h2_n5_%d" % t, tag=tag)
+            far = sb.tile([P, S], F32, name="h2_n5_%d" % t, tag=tag, align_bytes=64)
             nc.scalar.activation(far[:], h2[:].indirect(n5_l[:]), COPY)
-            nw[t] = sb.tile([P, S], F32, name="nw%d" % t)
+            nw[t] = sb.tile([P, S], F32, name="nw%d" % t, align_bytes=64)
             nc.vector.tensor_tensor(nw[t][:], h2[:, 0:S], far[:], ALU.max)
 
         larger(order[0], "far_a")
         larger(order[1], "far_b")
+        clear_page(3, "far_a")
         for i, t in enumerate(order):
             nc.scalar.activation(page[t][:].indirect(n4_l[:]), nw[t][:], COPY)
             nc.sync.dma_start(out_rows[:, t, :], page[t][:])

from contextlib import ExitStack

import concourse.mybir as mybir

K, T, S, G, H, U = 512, 1024, 256, 2048, 512, 1024
FLOPS = 3 * 2 * K * H * S

F32 = mybir.dt.float32
BF16 = mybir.dt.bfloat16
I32 = mybir.dt.int32
U32 = mybir.dt.uint32
U16 = mybir.dt.uint16
U8 = mybir.dt.uint8
FP8X4 = mybir.dt.float8_e4m3fn_x4
ALU = mybir.AluOpType
COPY = mybir.ActivationFunctionType.Copy

P = 128
HALF_P = P // 2
PACK = 4
LINE = 16
GATHER_W = S + 16
SCATTER_W = 2 * S
SIXTEENTH = 0.0625


def tile_picked_mhhzqsndminpags_none_po_kernel(
    tc, x_words, x_scales, d_words, d_scales, gs, offs, k1, hz, k2, n1, n2, n3, k3, n4, n5, out_0, out_1, out_2
):
    nc = tc.nc
    with ExitStack() as ctx:
        sb = ctx.enter_context(tc.tile_pool(name="sb", bufs=1))
        ps = ctx.enter_context(tc.psum_pool(name="ps", bufs=1))

        def load_list(src, name):
            lst = sb.tile(list(src.shape), U16, name=name)
            nc.sync.dma_start(lst[:], src)
            return lst

        def load_words(src, width, name):
            tab = sb.tile([P, width], I32, name=name, align_bytes=64)
            nc.sync.dma_start(tab[:], src[0].rearrange("p c r -> p (c r)").bitcast(I32))
            return tab

        def load_scales(src, width, name):
            tab = sb.tile([P, width], U8, name=name, align_bytes=64)
            rows = src[0].bitcast(I32).unsqueeze(1).broadcast_to([16, 8, width // 4])
            nc.scalar.dma_start(tab[:].bitcast(I32), rows)
            return tab

        def zeroed_bytes(width, name, tag):
            tile = sb.tile([P, width], U8, name=name, tag=tag, align_bytes=64)
            nc.vector.memset(tile[:].bitcast(I32), 0)
            return tile

        def place_scale_rows(dst, src, queues):
            for r in range(PACK):
                queues[r % len(queues)].dma_start(dst[r:P:32, :].bitcast(I32), src[8 * r : P : 32, :].bitcast(I32))

        def pick(dst, table, lst, first, count):
            nc.vector.tensor_copy(dst, table.indirect(lst[:, first // 16 : (first + count) // 16]))

        def deal(dst, src, run):
            nc.vector.tensor_copy(
                dst.rearrange("p a t (m i) -> p a m t i", i=run), src.rearrange("p a (m i) t -> p a m t i", i=run)
            )

        x_scale_tab = load_scales(x_scales, T, "x_scale_tab")
        d_scale_tab = load_scales(d_scales, G, "d_scale_tab")
        offs_l = load_list(offs, "offs_l")
        hz_l = load_list(hz, "hz_l")
        k1_l = load_list(k1, "k1_l")
        k2_l = load_list(k2, "k2_l")
        gs_t = sb.tile([P, PACK], F32, name="gs_t")
        nc.sync.dma_start(gs_t[:], gs.rearrange("(p t) o -> p (t o)", t=PACK))
        x_tab = load_words(x_words, T, "x_tab")
        n1_l = load_list(n1, "n1_l")
        n2_l = load_list(n2, "n2_l")
        n3_l = load_list(n3, "n3_l")
        d_tab = load_words(d_words, G, "d_tab")
        k3_l = load_list(k3, "k3_l")
        n5_l = load_list(n5, "n5_l")
        n4_l = load_list(n4, "n4_l")
        gs16 = sb.tile([P, PACK], F32, name="gs16")
        nc.scalar.activation(gs16[:], gs_t[:], COPY, scale=SIXTEENTH)
        minus_gs16 = sb.tile([P, PACK], F32, name="minus_gs16")
        nc.scalar.activation(minus_gs16[:], gs_t[:], COPY, scale=-SIXTEENTH)
        d_codes = d_tab[:].bitcast(U32)
        x_codes = x_tab[:].bitcast(U32)

        h_sc = zeroed_bytes(2 * H + 2 * S, "h_sc", "h_sc")
        w3_sc = zeroed_bytes(H, "w3_sc", "w3_sc")
        page = {}

        def clear_page(t, tag):
            page[t] = sb.tile([P, U], F32, name="page%d" % t, tag=tag, align_bytes=64)
            nc.vector.memset(page[t][:], 0.0)

        clear_page(2, "page2")
        clear_page(0, "page0")

        def deal_pair(dst, picked, pair, run):
            deal(dst, picked[:, :, :, 2 * pair : 2 * pair + 2], run)

        bx = sb.tile([P, 2 * S], U8, name="bx", align_bytes=64)
        pick(bx[:, 0:S], x_scale_tab[:], offs_l, 0, S)
        pick(bx[:, S : 2 * S], x_scale_tab[:], hz_l, 0, S)
        b12 = sb.tile([P, 2 * H], U8, name="b12", align_bytes=64)
        pick(b12[:, 0:H], d_scale_tab[:], k1_l, 0, H)
        pick(b12[:, H : 2 * H], d_scale_tab[:], k2_l, 0, H)
        h_b = sb.tile([P, 2 * H + 2 * S], U8, name="h_b", align_bytes=64)
        nc.vector.tensor_copy(h_b[:, 2 * H :].bitcast(I32), bx[:].bitcast(I32))
        deal_pair(
            h_b[:, 0:H].rearrange("p (a t m) -> p a t m", a=4, t=2),
            b12[:].rearrange("p (a m t) -> p a m t", a=4, t=PACK),
            0,
            LINE,
        )
        deal_pair(
            h_b[:, H : 2 * H].rearrange("p (a t m) -> p a t m", a=2, t=2),
            b12[:].rearrange("p (a m t) -> p a m t", a=2, t=PACK),
            1,
            LINE,
        )
        place_scale_rows(h_sc, h_b, (nc.sync, nc.scalar))

        gx = sb.tile([P, 2 * S], U32, name="gx", align_bytes=64)
        pick(gx[:, 0:S], x_codes, offs_l, 0, S)
        pick(gx[:, S : 2 * S], x_codes, hz_l, 0, S)
        h_w = sb.tile([P, 2 * H], U32, name="h_w", align_bytes=64)
        folded = h_w[:, 0:H].rearrange("p (a h t m) -> p a h t m", a=2, h=2, t=2)
        plain = h_w[:, H : 2 * H].rearrange("p (a t h m) -> p a t h m", a=2, t=2, h=2)

        def pick_half(half):
            tile = sb.tile([P, 2, HALF_P, PACK], U32, name="half_w", align_bytes=64)
            flat = tile[:].rearrange("p a m t -> p (a m t)")
            pick(flat[:, 0:S], d_codes, k1_l, half * S, S)
            pick(flat[:, S : 2 * S], d_codes, k2_l, half * S, S)
            deal_pair(folded[:, :, half, :, :], tile[:], 0, LINE // 4)
            deal_pair(plain[:, :, :, half, :], tile[:], 1, LINE // 4)

        def product(t):
            bank = ps.tile([P, S], F32, name="h_acc%d" % t)
            for a in range(2):
                first = (t // 2) * H + (2 * a + t % 2) * P
                nc.tensor.matmul_mx(
                    out=bank[:],
                    lhsT=h_w[:, first : first + P].bitcast(FP8X4),
                    lhsT_scale=h_sc[:, first : first + P],
                    rhs=gx[:, a * S : (a + 1) * S].bitcast(FP8X4),
                    rhs_scale=h_sc[:, 2 * H + a * S : 2 * H + (a + 1) * S],
                    start=(a == 0),
                    stop=(a == 1),
                )
            return bank

        h = [sb.tile([P, GATHER_W], F32, name="h%d" % t, align_bytes=64) for t in range(PACK)]
        pick_half(0)
        nc.scalar.copy(h[0][:, 0:S], product(0)[:])
        pick_half(1)
        for t in range(1, PACK):
            nc.vector.tensor_copy(h[t][:, 0:S], product(t)[:])

        ds, near, st = {}, {}, {}

        def send_n1(t, tag):
            ds[t] = sb.tile([P, SCATTER_W], F32, name="ds%d" % t, tag=tag, align_bytes=64)
            nc.scalar.activation(ds[t][:].indirect(n1_l[:]), h[t][:, 0:S], COPY)

        def fetch_n2(t, tag):
            near[t] = sb.tile([P, S], F32, name="h_n2_%d" % t, tag=tag, align_bytes=64)
            nc.scalar.activation(near[t][:], h[t][:].indirect(n2_l[:]), COPY)

        def smaller(t, tag):
            st[t] = sb.tile([P, GATHER_W], F32, name="st%d" % t, tag=tag, align_bytes=64)
            nc.vector.tensor_tensor(st[t][:, 0:S], ds[t][:, 0:S], near[t][:], ALU.min)

        def fetch_n3(t, first, count):
            far = sb.tile([P, count], F32, name="st_n3_%d_%d" % (t, first), align_bytes=64)
            nc.scalar.activation(far[:], st[t][:].indirect(n3_l[:, first // 16 : (first + count) // 16]), COPY)
            return far

        z_in = sb.tile([P, S, PACK], BF16, name="z_in", align_bytes=64)
        z_planes = sb.tile([P, PACK, S], BF16, name="z_planes", align_bytes=64)
        unfolded = sb.tile([P, 2, S], F32, name="unfolded", align_bytes=64)

        def unfold(half):
            diff = sb.tile([P, S], F32, name="diff%d" % half)
            nc.vector.tensor_tensor(diff[:], st[half][:, 0:S], fetch_n3(half, 0, S)[:], ALU.subtract)
            for t in range(2):
                nc.sync.dma_start(
                    unfolded[half * HALF_P : (half + 1) * HALF_P, t, :], diff[t * HALF_P : (t + 1) * HALF_P, :]
                )

        for t in range(2):
            send_n1(t, "ds%d" % t)
            fetch_n2(t, "near%d" % t)
            smaller(t, "st%d" % t)
        unfold(0)
        unfold(1)

        b3 = sb.tile([P, 1, P, PACK], U8, name="b3", tag="ds0", align_bytes=64)
        b3_flat = b3[:].rearrange("p a m t -> p (a m t)")
        for half in range(2):
            pick(b3_flat[:, half * S : (half + 1) * S], d_scale_tab[:], k3_l, half * S, S)
        b3_dealt = sb.tile([P, H], U8, name="b3_dealt", align_bytes=64)
        deal(b3_dealt[:].rearrange("p (a t m) -> p a t m", a=1, t=PACK), b3[:], LINE)
        place_scale_rows(w3_sc, b3_dealt, (nc.sync,))

        g3 = sb.tile([P, 1, P, PACK], U32, name="g3", tag="near1", align_bytes=64)
        g3_flat = g3[:].rearrange("p a m t -> p (a m t)")
        for half in range(2):
            pick(g3_flat[:, half * S : (half + 1) * S], d_codes, k3_l, half * S, S)
        w3 = sb.tile([P, H], U32, name="w3", align_bytes=64)
        deal(w3[:].rearrange("p (a t m) -> p a t m", a=1, t=PACK), g3[:], LINE // 4)

        z_words = sb.tile([P, S], U32, name="z_words", align_bytes=64)
        z_sc = sb.tile([P, S], U8, name="z_sc", align_bytes=64)
        order = (2, 0, 1, 3)
        banks = {t: ps.tile([P, S], F32, name="h2_acc%d" % t) for t in order}
        weighted = {}

        def weigh(t, tag):
            weighted[t] = sb.tile([P, S], F32, name="weighted%d" % t, tag=tag, align_bytes=64)
            nc.vector.tensor_scalar(weighted[t][:], st[t][:, 0:S], gs16[:, t : t + 1], None, ALU.mult)

        def finish_z(t, first, count):
            toks = slice(first, first + count)
            nc.vector.scalar_tensor_tensor(
                z_planes[:, t, toks],
                fetch_n3(t, first, count)[:],
                minus_gs16[:, t : t + 1],
                weighted[t][:, toks],
                ALU.mult,
                ALU.add,
            )

        send_n1(2, "ds1")
        fetch_n2(2, "near2")
        smaller(2, "st2")
        clear_page(1, "near2")
        send_n1(3, "h2")
        fetch_n2(3, "near3")
        for t in range(2):
            nc.vector.tensor_scalar(z_planes[:, t, :], unfolded[:, t, :], gs16[:, t : t + 1], None, ALU.mult)
        smaller(3, "unfolded")
        weigh(2, "near3")
        weigh(3, "weighted3")
        finish_z(2, 0, S)
        finish_z(3, 0, P)
        finish_z(3, P, P)
        for half in range(2):
            toks = slice(half * P, (half + 1) * P)
            nc.vector.tensor_copy(
                z_in[:, toks, :].rearrange("p (c i) t -> p c t i", i=4),
                z_planes[:, :, toks].rearrange("p t (c i) -> p c t i", i=4),
            )
        for half in range(2):
            toks = slice(half * P, (half + 1) * P)
            nc.vector.quantize_mx(
                out=z_words[:, toks].bitcast(FP8X4),
                scales=z_sc[:, toks],
                in_=z_in[:, toks, :].rearrange("p c t -> p (c t)"),
            )
        for t in order:
            cols = slice(t * P, (t + 1) * P)
            for half in range(2):
                toks = slice(half * P, (half + 1) * P)
                nc.tensor.matmul_mx(
                    out=banks[t][:, toks],
                    lhsT=w3[:, cols].bitcast(FP8X4),
                    lhsT_scale=w3_sc[:, cols],
                    rhs=z_words[:, toks].bitcast(FP8X4),
                    rhs_scale=z_sc[:, toks],
                    start=True,
                    stop=True,
                )

        y_in = sb.tile([P, U, PACK], BF16, name="y_in", align_bytes=64)
        y_words = sb.tile([P, U], I32, name="y_words", align_bytes=64)
        y_sc = sb.tile([P, U], U8, name="y_sc", align_bytes=64)
        out_rows = out_0.rearrange("(p t) c -> p t c", t=PACK)
        out_words = out_1[0].rearrange("p c r -> p (c r)").bitcast(I32)
        nw = {}

        def larger(t, tag):
            h2 = sb.tile([P, GATHER_W], F32, name="h2_%d" % t)
            nc.vector.tensor_scalar(h2[:, 0:S], banks[t][:], SIXTEENTH, None, ALU.mult)
            far = sb.tile([P, S], F32, name="h2_n5_%d" % t, tag=tag, align_bytes=64)
            nc.scalar.activation(far[:], h2[:].indirect(n5_l[:]), COPY)
            nw[t] = sb.tile([P, S], F32, name="nw%d" % t, align_bytes=64)
            nc.vector.tensor_tensor(nw[t][:], h2[:, 0:S], far[:], ALU.max)

        larger(order[0], "far_a")
        larger(order[1], "far_b")
        clear_page(3, "far_a")
        for i, t in enumerate(order):
            nc.scalar.activation(page[t][:].indirect(n4_l[:]), nw[t][:], COPY)
            nc.sync.dma_start(out_rows[:, t, :], page[t][:])
            if t != order[-1]:
                nc.vector.tensor_copy(y_in[:, :, t], page[t][:])
            if i + 2 < PACK:
                larger(order[i + 2], "nw%d" % t)
        last = order[-1]
        pieces = (slice(0, U // 2), slice(U // 2, 3 * U // 4), slice(3 * U // 4, U))
        nc.vector.tensor_copy(y_in[:, pieces[0], last], page[last][:, pieces[0]])
        for cols in pieces[1:]:
            nc.scalar.copy(y_in[:, cols, last], page[last][:, cols])
        for cols in pieces:
            nc.vector.quantize_mx(
                out=y_words[:, cols].bitcast(FP8X4),
                scales=y_sc[:, cols],
                in_=y_in[:, cols, :].rearrange("p c t -> p (c t)"),
            )
            nc.sync.dma_start(out_words[:, cols], y_words[:, cols])
        for q in range(4):
            queue = nc.scalar if q % 2 == 0 else nc.sync
            queue.dma_start(out_2[0][4 * q : 4 * q + 4, :].bitcast(I32), y_sc[32 * q : 32 * q + 4, :].bitcast(I32))
